import numpy as np
import ml_dtypes


def mxq(x, axis, fmt="e4m3"):
    dtype, down = {"e4m3": (ml_dtypes.float8_e4m3fn, 7), "e5m2": (ml_dtypes.float8_e5m2, 14)}[fmt]
    v = np.moveaxis(np.asarray(x, np.float32).astype(ml_dtypes.bfloat16).astype(np.float64), axis, -1)
    blocks = v.reshape(v.shape[:-1] + (-1, 32))
    amax = np.abs(blocks).max(-1, keepdims=True)
    byte = np.maximum(np.where(amax > 0, np.frexp(amax)[1] - 1 + 127, 0) - down, 1)
    scale = np.exp2(byte - 127.0)
    codes = (blocks / scale).astype(np.float32).astype(dtype).astype(np.float64)
    return np.moveaxis((codes * scale).reshape(v.shape), -1, axis)


WIDE = False


def mx_kscale(k):
    if not WIDE:
        return np.ones(k)
    levels = np.array([10, -10, 5, -5, 0])
    if k % 512:
        return np.exp2(np.random.permutation(np.resize(levels, k // 32))).repeat(32)
    a = np.empty((k // 512, 16))
    for p in range(k // 512):
        a[p, :8] = np.random.permutation(np.resize(levels, 8))
        for g in range(8):
            far = levels[np.abs(levels - a[p, g]) >= 10]
            a[p, g + 8] = far[np.random.randint(len(far))]
    return np.exp2(a.ravel()).repeat(32)


def f64(x):
    return np.asarray(x).astype(np.float64)


def striped(idx):
    return np.tile(idx.reshape(-1, 16).T, (8, 1)).astype(np.uint16)


def unstriped(offs):
    return offs[:16].T.reshape(-1).astype(np.int64)


def striped8(idx):
    return np.concatenate([x.reshape(-1, 16).T for x in idx]).astype(np.uint16)


def runs(offs, k):
    lists = np.stack([offs[16 * r : 16 * r + 16].T.reshape(-1) for r in range(8)]).astype(np.int64)
    return lists[np.arange(k) % 512 // 64]


def pack_weight(w):
    k, n = w.shape
    w = f64(np.asarray(w, np.float32).astype(ml_dtypes.bfloat16)).reshape(k // 32, 32, n)
    amax = np.abs(w).max(1)
    byte = np.clip(np.where(amax > 0, np.frexp(amax)[1] - 1 + 127 - 7, 1), 1, 254)
    scaled = (w * np.exp2(127.0 - byte)[:, None, :]).reshape(k, n).astype(np.float32)
    words = np.ascontiguousarray(scaled.reshape(k // 512, 128, 4, n).transpose(0, 1, 3, 2)).astype(ml_dtypes.float8_e4m3fn).view(np.uint8)
    return words, np.ascontiguousarray(byte.astype(np.uint8).reshape(k // 512, 16, n))


def unpack_weight(words, scales):
    g, p, n, _ = words.shape
    vals = np.ascontiguousarray(words).view(ml_dtypes.float8_e4m3fn).astype(np.float64) * np.repeat(np.exp2(scales.astype(np.float64) - 127.0), 8, axis=1)[..., None]
    return vals.transpose(0, 1, 3, 2).reshape(g * 512, n)


E2M1 = np.array([0.0, 0.5, 1.0, 1.5, 2.0, 3.0, 4.0, 6.0, -0.0, -0.5, -1.0, -1.5, -2.0, -3.0, -4.0, -6.0])


def pack_fp4(w):
    k, n = w.shape
    w = f64(np.asarray(w, np.float32).astype(ml_dtypes.bfloat16)).reshape(k // 32, 32, n)
    amax = np.abs(w).max(1)
    mant, ex = np.frexp(amax / 6.0)
    byte = np.clip(np.where(amax > 0, np.where(mant > 0.5, ex, ex - 1) + 127, 1), 1, 254)
    scaled = (w * np.exp2(127.0 - byte)[:, None, :]).reshape(k, n).astype(np.float32)
    c = np.ascontiguousarray(scaled.reshape(k // 512, 128, 4, n).transpose(0, 1, 3, 2)).astype(ml_dtypes.float4_e2m1fn).view(np.uint8) & 0xF
    words = (c[..., 0::2] | (c[..., 1::2] << 4)).reshape(k // 512, 128, 2 * n)
    return np.ascontiguousarray(words), np.ascontiguousarray(byte.astype(np.uint8).reshape(k // 512, 16, n))


def unpack_fp4(words, scales):
    g, _, n = scales.shape
    words = np.ascontiguousarray(words).reshape(g, 128, n, 2)
    nib = np.empty((g, 128, n, 4), np.uint8)
    nib[..., 0::2] = words & 0xF
    nib[..., 1::2] = words >> 4
    vals = E2M1[nib] * np.repeat(np.exp2(scales.astype(np.float64) - 127.0), 8, axis=1)[..., None]
    return vals.transpose(0, 1, 3, 2).reshape(g * 512, n)


def sigmoid(v):
    return 1.0 / (1.0 + np.exp(-np.maximum(v, -700.0)))


K, T, S, H, W, G = 512, 1024, 256, 512, 128, 2048


def setup_inputs():
    n = np.random.standard_normal
    s = mx_kscale(K)[:, None]
    packed_xT = pack_weight(n((K, T)) * s)
    packed_w1 = pack_fp4(n((K, H)) / np.sqrt(K) / s)
    packed_dT = pack_weight(n((K, G)) / s)
    perm = np.random.permutation(S)
    return {
        "x_words": packed_xT[0],
        "x_scales": packed_xT[1],
        "w1_words": packed_w1[0],
        "w1_scales": packed_w1[1],
        "gs": (np.random.uniform(0.5, 1.5, (K, 1)) * s).astype(np.float32),
        "d_words": packed_dT[0],
        "d_scales": packed_dT[1],
        "sl": np.random.uniform(1.0, 2.0, (H, 1)).astype(np.float32),
        "th": (0.5 * n((H, 1))).astype(np.float32),
        "offs": striped(np.random.permutation(T)[:S]),
        "n1": striped(perm[:W]),
        "n2": striped(perm[W:]),
        "n3": striped(np.random.permutation(S)),
        "k1": striped8(np.random.randint(0, G, (8, H))),
        "k2": striped8(np.random.randint(0, G, (8, H))),
        "two": striped(np.random.permutation(T)[:S]),
        "n4": striped8(np.stack([np.random.permutation(S) for _ in range(8)])),
        "n5": striped8(np.stack([np.random.permutation(S) for _ in range(8)])),
    }


def reference(x_words, x_scales, w1_words, w1_scales, gs, d_words, d_scales, sl, th, offs, n1, n2, n3, k1, k2, two, n4, n5):
    d_k1 = unpack_weight(d_words, d_scales)[np.arange(K)[:, None], runs(k1, K)]
    xq = unpack_weight(x_words, x_scales)[:, unstriped(offs)]
    y = unpack_fp4(w1_words, w1_scales).T @ xq
    pa = y[:, unstriped(n1)]
    pb = y[:, unstriped(n2)]
    rb = pa - pb
    ra = pa + pb
    ds = np.zeros((H, S))
    ds[:, unstriped(n1)] = ra
    dt = ds.copy()
    dt[:, unstriped(n2)] = rb
    z = f64(gs) * (np.maximum(dt, dt[:, unstriped(n3)]))
    d_k2 = unpack_weight(d_words, d_scales)[np.arange(K)[:, None], runs(k2, K)]
    x_two = unpack_weight(x_words, x_scales)[:, unstriped(two)]
    h = 0.0625 * ((d_k1.T @ mxq(z, 0, "e4m3") + d_k2.T @ x_two))
    st = h - (h[np.arange(H)[:, None], runs(n4, H)])
    sg = sigmoid(f64(sl) * (st[np.arange(H)[:, None], runs(n5, H)] - f64(th)))
    return h * sg

@@ -1,0 +1,247 @@
+from contextlib import ExitStack
+
+import concourse.mybir as mybir
+
+FLOPS = 402653184
+
+F32 = mybir.dt.float32
+BF16 = mybir.dt.bfloat16
+I32 = mybir.dt.int32
+U32 = mybir.dt.uint32
+U16 = mybir.dt.uint16
+U8 = mybir.dt.uint8
+FP8X4 = mybir.dt.float8_e4m3fn_x4
+FP4X4 = mybir.dt.float4_e2m1fn_x4
+ALU = mybir.AluOpType
+ACT = mybir.ActivationFunctionType
+
+P = 128
+PACK = 4
+T, S, H, W, G = 1024, 256, 512, 128, 2048
+HALF = S // 2
+
+
+def tile_picked_cmixhaarhehq_none_p_kernel(
+    tc, x_words, x_scales, w1_words, w1_scales, gs, d_words, d_scales, sl, th,
+    offs, n1, n2, n3, k1, k2, two, n4, n5, out,
+):
+    nc = tc.nc
+    with ExitStack() as ctx:
+        lists = ctx.enter_context(tc.tile_pool(name="lists", bufs=1))
+        keep = ctx.enter_context(tc.tile_pool(name="keep", bufs=1))
+        shared = ctx.enter_context(tc.tile_pool(name="shared", bufs=1))
+        psum = ctx.enter_context(tc.psum_pool(name="psum", bufs=1))
+
+        def load_list(src, name):
+            tile = lists.tile([P, src.shape[1]], U16, name=name)
+            nc.sync.dma_start(tile[:], src)
+            return tile
+
+        def load_rows(src, name):
+            tile = keep.tile([P, PACK], F32, name=name)
+            nc.sync.dma_start(tile[:], src.rearrange("(p t) o -> p (t o)", t=PACK))
+            return tile
+
+        def deal(engine_copy, dst, src, run):
+            engine_copy(
+                dst.rearrange("p (t b i) -> p b t i", t=PACK, i=run),
+                src.rearrange("p (b i t) -> p b t i", t=PACK, i=run),
+            )
+
+        xs_win = keep.tile([P, T], U8, name="xs_win")
+        w1s_raw = shared.tile([P, H], U8, name="w1s_raw", offset=6656)
+        ds_win = keep.tile([P, G], U8, name="ds_win")
+        ds_moved = shared.tile([P, H], U8, name="ds_moved", offset=0)
+        nc.vector.memset(xs_win[:, :384].bitcast(I32), 0)
+        nc.gpsimd.memset(xs_win[:, 384:].bitcast(I32), 0)
+        nc.vector.memset(w1s_raw[:].bitcast(I32), 0)
+
+        offs_t = load_list(offs, "offs_t")
+        two_t = load_list(two, "two_t")
+        w1w_raw = keep.tile([P, 2 * H], U8, name="w1w_raw")
+        nc.sync.dma_start(w1w_raw[:].bitcast(I32), w1_words[0].bitcast(I32))
+        n1_t = load_list(n1, "n1_t")
+        xw_win = keep.tile([P, T], U32, name="xw_win")
+        nc.sync.dma_start(xw_win[:].bitcast(I32), x_words[0].rearrange("p n t -> p (n t)").bitcast(I32))
+        for q in range(4):
+            queue = nc.sync if q == 0 else nc.scalar
+            queue.dma_start(xs_win[32 * q : 32 * q + 4, :].bitcast(I32), x_scales[0, 4 * q : 4 * q + 4, :].bitcast(I32))
+        for q in range(4):
+            nc.sync.dma_start(w1s_raw[32 * q : 32 * q + 4, :].bitcast(I32), w1_scales[0, 4 * q : 4 * q + 4, :].bitcast(I32))
+        n2_t = load_list(n2, "n2_t")
+        nc.vector.memset(ds_win[:].bitcast(I32), 0)
+        nc.vector.memset(ds_moved[:].bitcast(I32), 0)
+        nc.sync.dma_start(ds_win[0:P:8, :].bitcast(I32), d_scales[0].bitcast(I32))
+        k1_t = load_list(k1, "k1_t")
+        k2_t = load_list(k2, "k2_t")
+        n3_t = load_list(n3, "n3_t")
+        gs_t = load_rows(gs, "gs_t")
+        dw_win = keep.tile([P, G], U32, name="dw_win")
+        nc.sync.dma_start(dw_win[:].bitcast(I32), d_words[0].rearrange("p n t -> p (n t)").bitcast(I32))
+        n4_t = load_list(n4, "n4_t")
+        n5_t = load_list(n5, "n5_t")
+        sl_t = load_rows(sl, "sl_t")
+        th_t = load_rows(th, "th_t")
+
+        w1w = keep.tile([P, 2 * H], U8, name="w1w", align_bytes=64)
+        deal(nc.scalar.copy, w1w[:].bitcast(U16), w1w_raw[:].bitcast(U16), 8)
+        w1s_first = keep.tile([P, P], U8, name="w1s_first", align_bytes=64)
+        w1s_rest = keep.tile([P, H - P], U8, name="w1s_rest", align_bytes=64)
+        xq_s = keep.tile([P, S], U8, name="xq_s", align_bytes=64)
+        xq_w = keep.tile([P, S], U32, name="xq_w", align_bytes=64)
+        nc.vector.tensor_copy(xq_s[:], xs_win[:].indirect(offs_t[:]))
+        xt_s = shared.tile([P, S], U8, name="xt_s", align_bytes=64, offset=6656)
+        xt_w = shared.tile([P, S], U32, name="xt_w", align_bytes=64, offset=6912)
+        nc.vector.tensor_copy(xq_w[:], xw_win[:].indirect(offs_t[:]))
+        w1s_by_t = w1s_raw[:].rearrange("p (m t) -> p t m", t=PACK)
+        nc.vector.tensor_copy(w1s_first[:], w1s_by_t[:, 0, :])
+        nc.vector.tensor_copy(
+            w1s_rest[:].rearrange("p (t b i) -> p b t i", t=PACK - 1, i=16),
+            w1s_by_t[:, 1:, :].rearrange("p t (b i) -> p b t i", i=16),
+        )
+
+        y = []
+        for t in range(PACK):
+            bank = psum.tile([P, S], F32, name="y_bank", tag=f"a{t}")
+            nc.tensor.matmul_mx(
+                out=bank[:],
+                lhsT=w1w[:, 2 * P * t : 2 * P * (t + 1)].bitcast(FP4X4),
+                lhsT_scale=w1s_first[:] if t == 0 else w1s_rest[:, P * (t - 1) : P * t],
+                rhs=xq_w[:].bitcast(FP8X4),
+                rhs_scale=xq_s[:],
+                start=True,
+                stop=True,
+            )
+            y_t = shared.tile([P, S], F32, name=f"y{t}", offset=(8192, 4608, 5632, 2048)[t])
+            if t == 0:
+                nc.scalar.copy(y_t[:], bank[:])
+            else:
+                nc.vector.tensor_copy(y_t[:], bank[:])
+            y.append(y_t)
+
+        haar = []
+        dt = [keep.tile([P, 2 * S], F32, name=f"dt{t}") for t in range(PACK)]
+        for t in range(PACK):
+            pa, pb = dt[t][:, S : S + W], dt[t][:, S + W :]
+            nc.scalar.activation(pa, y[t][:].indirect(n1_t[:]), ACT.Copy)
+            nc.scalar.activation(pb, y[t][:].indirect(n2_t[:]), ACT.Copy)
+            haar_t = keep.tile([P, 2, W], F32, name=f"haar{t}")
+            nc.vector.tensor_tensor(haar_t[:, 0, :], pa, pb, ALU.add)
+            nc.vector.tensor_tensor(haar_t[:, 1, :], pa, pb, ALU.subtract)
+            haar.append(haar_t)
+
+        nc.vector.tensor_copy(xt_w[:], xw_win[:].indirect(two_t[:]))
+        nc.vector.tensor_copy(xt_s[:], xs_win[:].indirect(two_t[:]))
+
+        for m, k_t in enumerate((k1_t, k2_t)):
+            ds_got = shared.tile([P, H], U8, name=f"ds_got{m}", offset=(4608, 5632)[m])
+            nc.vector.tensor_copy(ds_got[:], ds_win[:].indirect(k_t[:]))
+            for r in range(4):
+                nc.sync.dma_start(ds_moved[4 * m + r : P : 32, :].bitcast(I32), ds_got[8 * r : P : 32, :].bitcast(I32))
+        dw = []
+        for m, k_t in enumerate((k1_t, k2_t)):
+            got = shared.tile([P, H], U32, name=f"dw_got{m}", offset=(512, 2560)[m])
+            nc.vector.tensor_copy(got[:], dw_win[:].indirect(k_t[:]))
+            dealt = keep.tile([P, H], U32, name=f"dw_dealt{m}", align_bytes=64)
+            deal(nc.vector.tensor_copy, dealt[:], got[:], 4)
+            dw.append(dealt)
+        ds_plane = keep.tile([P, H], U8, name="ds_plane", align_bytes=64)
+        deal(nc.vector.tensor_copy, ds_plane[:], ds_moved[:], 16)
+        neg_bias = keep.tile([P, PACK], F32, name="neg_bias")
+        nc.vector.scalar_tensor_tensor(neg_bias[:], sl_t[:], -1.0, th_t[:], ALU.mult, ALU.mult)
+
+        h_bank = [[psum.tile([P, HALF], F32, name="h_bank", tag=f"{'ab'[u]}{t}") for t in range(PACK)] for u in range(2)]
+
+        def h_pass(u, t, m, words, scales):
+            nc.tensor.matmul_mx(
+                out=h_bank[u][t][:],
+                lhsT=dw[m][:, P * t : P * (t + 1)].bitcast(FP8X4),
+                lhsT_scale=ds_plane[4 * m : P, P * t : P * (t + 1)],
+                rhs=words.bitcast(FP8X4),
+                rhs_scale=scales,
+                start=(m == 1),
+                stop=(m == 0),
+            )
+
+        for u in range(2):
+            for t in range(PACK):
+                cols = slice(u * HALF, (u + 1) * HALF)
+                h_pass(u, t, 1, xt_w[:, cols], xt_s[:, cols])
+
+        h_win = [keep.tile([P, 2 * S], F32, name=f"h_win{t}") for t in range(PACK)]
+        dt_n3 = [h_win[t][:, S:] for t in range(PACK)]
+        larger = shared.tile([P, PACK * S], F32, name="larger", offset=0)
+        z = [keep.tile([P, HALF, PACK], BF16, name=f"z{u}", align_bytes=64) for u in range(2)]
+
+        def scatter(t, side):
+            nc.scalar.activation(dt[t][:].indirect((n1_t, n2_t)[side][:]), haar[t][:, side, :], ACT.Copy)
+
+        def fetch_n3(t, lo, hi):
+            nc.scalar.activation(dt_n3[t][:, lo:hi], dt[t][:].indirect(n3_t[:, lo // 16 : hi // 16]), ACT.Copy)
+
+        def take_larger(t, lo, hi):
+            nc.vector.tensor_tensor(larger[:, t * S + lo : t * S + hi], dt[t][:, lo:hi], dt_n3[t][:, lo:hi], ALU.max)
+
+        def weigh(t, u):
+            nc.vector.tensor_scalar(z[u][:, :, t], larger[:, t * S + u * HALF : t * S + (u + 1) * HALF], gs_t[:, t : t + 1], None, ALU.mult)
+
+        scatter(0, 0)
+        scatter(1, 0)
+        scatter(0, 1)
+        scatter(1, 1)
+        scatter(2, 0)
+        fetch_n3(0, 0, S)
+        scatter(2, 1)
+        fetch_n3(1, 0, S)
+        scatter(3, 0)
+        fetch_n3(2, 0, S)
+        scatter(3, 1)
+        fetch_n3(3, 0, HALF)
+        fetch_n3(3, HALF, S)
+        for t in range(PACK - 1):
+            take_larger(t, 0, S)
+            weigh(t, 0)
+            weigh(t, 1)
+        take_larger(3, 0, HALF)
+        take_larger(3, HALF, S)
+        weigh(3, 0)
+        weigh(3, 1)
+
+        z_mx = []
+        for u in range(2):
+            z_w = keep.tile([P, HALF], U32, name=f"z_w{u}", align_bytes=64)
+            z_s = keep.tile([P, HALF], U8, name=f"z_s{u}", align_bytes=64)
+            nc.vector.quantize_mx(out=z_w[:].bitcast(FP8X4), scales=z_s[:], in_=z[u][:].rearrange("p c t -> p (c t)"))
+            z_mx.append((z_w, z_s))
+        for t in range(PACK):
+            for u in range(2):
+                h_pass(u, t, 0, z_mx[u][0][:], z_mx[u][1][:])
+                cols = slice(u * HALF, (u + 1) * HALF)
+                if t == 0:
+                    nc.scalar.activation(h_win[t][:, cols], h_bank[u][t][:], ACT.Copy, scale=0.0625)
+                else:
+                    nc.vector.tensor_scalar(h_win[t][:, cols], h_bank[u][t][:], 0.0625, None, ALU.mult)
+
+        out_rows = out.rearrange("(p t) c -> p t c", t=PACK)
+        st_win = [keep.tile([P, 2 * S], F32, name=f"st_win{t}") for t in range(PACK)]
+
+        def make_st(t):
+            nc.scalar.activation(st_win[t][:, S:], h_win[t][:].indirect(n4_t[:]), ACT.Copy)
+            nc.vector.tensor_tensor(st_win[t][:, :S], h_win[t][:, :S], st_win[t][:, S:], ALU.subtract)
+
+        def finish(t, lo, hi):
+            sg = keep.tile([P, hi - lo], F32, name=f"sg{t}_{lo}")
+            nc.scalar.activation(
+                sg[:], st_win[t][:].indirect(n5_t[:, lo // 16 : hi // 16]), ACT.Sigmoid,
+                bias=neg_bias[:, t : t + 1], scale=sl_t[:, t : t + 1],
+            )
+            res = keep.tile([P, hi - lo], F32, name=f"res{t}_{lo}")
+            nc.vector.tensor_tensor(res[:], h_win[t][:, lo:hi], sg[:], ALU.mult)
+            nc.sync.dma_start(out_rows[:, t, lo:hi], res[:])
+
+        make_st(0)
+        for t in range(PACK - 1):
+            make_st(t + 1)
+            finish(t, 0, S)
+        finish(PACK - 1, 0, HALF)
+        finish(PACK - 1, HALF, S)

@@ -83,6 +83,11 @@ def tile_picked_cmixhaarhehq_none_p_kernel(
         sl_t = load_rows(sl, "sl_t")
         th_t = load_rows(th, "th_t")
 
+        warm_in = keep.tile([P, 1], F32, name="warm_in")
+        warm_out = keep.tile([P, 1], F32, name="warm_out")
+        nc.gpsimd.memset(warm_in[:], 0.0)
+        nc.scalar.activation(warm_out[:], warm_in[:], ACT.Sigmoid)
+
         w1w = keep.tile([P, 2 * H], U8, name="w1w", align_bytes=64)
         deal(nc.scalar.copy, w1w[:].bitcast(U16), w1w_raw[:].bitcast(U16), 8)
         w1s_first = keep.tile([P, P], U8, name="w1s_first", align_bytes=64)

@@ -19,6 +19,18 @@ P = 128
 PACK = 4
 T, S, H, W, G = 1024, 256, 512, 128, 2048
 HALF = S // 2
+LAST = PACK - 1
+QUADRANT = 32
+GROUP = 16
+LINE = 16
+XS_ZEROED_BY_VECTOR = 384
+
+DS_MOVED_AT = LARGER_AT = 0
+DW_GOT_AT = (512, 2560)
+DS_GOT_AT = (4608, 5632)
+Y_AT = (8192, DS_GOT_AT[0], DS_GOT_AT[1], 2048)
+W1S_RAW_AT = XT_S_AT = 6656
+XT_W_AT = XT_S_AT + S
 
 
 def tile_picked_cmixhaarhehq_none_p_kernel(
@@ -42,6 +54,10 @@ def tile_picked_cmixhaarhehq_none_p_kernel(
             nc.sync.dma_start(tile[:], src.rearrange("(p t) o -> p (t o)", t=PACK))
             return tile
 
+        def load_scale_rows(queue, tile, scales, q):
+            rows = tile[QUADRANT * q : QUADRANT * q + PACK, :]
+            queue.dma_start(rows.bitcast(I32), scales[0, PACK * q : PACK * (q + 1), :].bitcast(I32))
+
         def deal(engine_copy, dst, src, run):
             engine_copy(
                 dst.rearrange("p (t b i) -> p b t i", t=PACK, i=run),
@@ -49,11 +65,11 @@ def tile_picked_cmixhaarhehq_none_p_kernel(
             )
 
         xs_win = keep.tile([P, T], U8, name="xs_win")
-        w1s_raw = shared.tile([P, H], U8, name="w1s_raw", offset=6656)
+        w1s_raw = shared.tile([P, H], U8, name="w1s_raw", offset=W1S_RAW_AT)
         ds_win = keep.tile([P, G], U8, name="ds_win")
-        ds_moved = shared.tile([P, H], U8, name="ds_moved", offset=0)
-        nc.vector.memset(xs_win[:, :384].bitcast(I32), 0)
-        nc.gpsimd.memset(xs_win[:, 384:].bitcast(I32), 0)
+        ds_moved = shared.tile([P, H], U8, name="ds_moved", offset=DS_MOVED_AT)
+        nc.vector.memset(xs_win[:, :XS_ZEROED_BY_VECTOR].bitcast(I32), 0)
+        nc.gpsimd.memset(xs_win[:, XS_ZEROED_BY_VECTOR:].bitcast(I32), 0)
         nc.vector.memset(w1s_raw[:].bitcast(I32), 0)
 
         offs_t = load_list(offs, "offs_t")
@@ -63,11 +79,10 @@ def tile_picked_cmixhaarhehq_none_p_kernel(
         n1_t = load_list(n1, "n1_t")
         xw_win = keep.tile([P, T], U32, name="xw_win")
         nc.sync.dma_start(xw_win[:].bitcast(I32), x_words[0].rearrange("p n t -> p (n t)").bitcast(I32))
-        for q in range(4):
-            queue = nc.sync if q == 0 else nc.scalar
-            queue.dma_start(xs_win[32 * q : 32 * q + 4, :].bitcast(I32), x_scales[0, 4 * q : 4 * q + 4, :].bitcast(I32))
-        for q in range(4):
-            nc.sync.dma_start(w1s_raw[32 * q : 32 * q + 4, :].bitcast(I32), w1_scales[0, 4 * q : 4 * q + 4, :].bitcast(I32))
+        for q in range(PACK):
+            load_scale_rows(nc.sync if q == 0 else nc.scalar, xs_win, x_scales, q)
+        for q in range(PACK):
+            load_scale_rows(nc.sync, w1s_raw, w1_scales, q)
         n2_t = load_list(n2, "n2_t")
         nc.vector.memset(ds_win[:].bitcast(I32), 0)
         nc.vector.memset(ds_moved[:].bitcast(I32), 0)
@@ -89,20 +104,20 @@ def tile_picked_cmixhaarhehq_none_p_kernel(
         nc.scalar.activation(warm_out[:], warm_in[:], ACT.Sigmoid)
 
         w1w = keep.tile([P, 2 * H], U8, name="w1w", align_bytes=64)
-        deal(nc.scalar.copy, w1w[:].bitcast(U16), w1w_raw[:].bitcast(U16), 8)
+        deal(nc.scalar.copy, w1w[:].bitcast(U16), w1w_raw[:].bitcast(U16), LINE // 2)
         w1s_first = keep.tile([P, P], U8, name="w1s_first", align_bytes=64)
         w1s_rest = keep.tile([P, H - P], U8, name="w1s_rest", align_bytes=64)
         xq_s = keep.tile([P, S], U8, name="xq_s", align_bytes=64)
         xq_w = keep.tile([P, S], U32, name="xq_w", align_bytes=64)
         nc.vector.tensor_copy(xq_s[:], xs_win[:].indirect(offs_t[:]))
-        xt_s = shared.tile([P, S], U8, name="xt_s", align_bytes=64, offset=6656)
-        xt_w = shared.tile([P, S], U32, name="xt_w", align_bytes=64, offset=6912)
+        xt_s = shared.tile([P, S], U8, name="xt_s", align_bytes=64, offset=XT_S_AT)
+        xt_w = shared.tile([P, S], U32, name="xt_w", align_bytes=64, offset=XT_W_AT)
         nc.vector.tensor_copy(xq_w[:], xw_win[:].indirect(offs_t[:]))
         w1s_by_t = w1s_raw[:].rearrange("p (m t) -> p t m", t=PACK)
         nc.vector.tensor_copy(w1s_first[:], w1s_by_t[:, 0, :])
         nc.vector.tensor_copy(
-            w1s_rest[:].rearrange("p (t b i) -> p b t i", t=PACK - 1, i=16),
-            w1s_by_t[:, 1:, :].rearrange("p t (b i) -> p b t i", i=16),
+            w1s_rest[:].rearrange("p (t b i) -> p b t i", t=PACK - 1, i=LINE),
+            w1s_by_t[:, 1:, :].rearrange("p t (b i) -> p b t i", i=LINE),
         )
 
         y = []
@@ -117,7 +132,7 @@ def tile_picked_cmixhaarhehq_none_p_kernel(
                 start=True,
                 stop=True,
             )
-            y_t = shared.tile([P, S], F32, name=f"y{t}", offset=(8192, 4608, 5632, 2048)[t])
+            y_t = shared.tile([P, S], F32, name=f"y{t}", offset=Y_AT[t])
             if t == 0:
                 nc.scalar.copy(y_t[:], bank[:])
             else:
@@ -139,93 +154,96 @@ def tile_picked_cmixhaarhehq_none_p_kernel(
         nc.vector.tensor_copy(xt_s[:], xs_win[:].indirect(two_t[:]))
 
         for m, k_t in enumerate((k1_t, k2_t)):
-            ds_got = shared.tile([P, H], U8, name=f"ds_got{m}", offset=(4608, 5632)[m])
+            ds_got = shared.tile([P, H], U8, name=f"ds_got{m}", offset=DS_GOT_AT[m])
             nc.vector.tensor_copy(ds_got[:], ds_win[:].indirect(k_t[:]))
-            for r in range(4):
-                nc.sync.dma_start(ds_moved[4 * m + r : P : 32, :].bitcast(I32), ds_got[8 * r : P : 32, :].bitcast(I32))
+            for r in range(PACK):
+                nc.sync.dma_start(
+                    ds_moved[PACK * m + r : P : QUADRANT, :].bitcast(I32), ds_got[8 * r : P : QUADRANT, :].bitcast(I32)
+                )
         dw = []
         for m, k_t in enumerate((k1_t, k2_t)):
-            got = shared.tile([P, H], U32, name=f"dw_got{m}", offset=(512, 2560)[m])
+            got = shared.tile([P, H], U32, name=f"dw_got{m}", offset=DW_GOT_AT[m])
             nc.vector.tensor_copy(got[:], dw_win[:].indirect(k_t[:]))
             dealt = keep.tile([P, H], U32, name=f"dw_dealt{m}", align_bytes=64)
-            deal(nc.vector.tensor_copy, dealt[:], got[:], 4)
+            deal(nc.vector.tensor_copy, dealt[:], got[:], LINE // 4)
             dw.append(dealt)
         ds_plane = keep.tile([P, H], U8, name="ds_plane", align_bytes=64)
-        deal(nc.vector.tensor_copy, ds_plane[:], ds_moved[:], 16)
+        deal(nc.vector.tensor_copy, ds_plane[:], ds_moved[:], LINE)
         neg_bias = keep.tile([P, PACK], F32, name="neg_bias")
         nc.vector.scalar_tensor_tensor(neg_bias[:], sl_t[:], -1.0, th_t[:], ALU.mult, ALU.mult)
 
-        h_bank = [[psum.tile([P, HALF], F32, name="h_bank", tag=f"{'ab'[u]}{t}") for t in range(PACK)] for u in range(2)]
+        h_groups = [(0, 0, HALF), (0, HALF, S)] + [(t, 0, S) for t in range(1, PACK)]
+        h_bank = {
+            (t, lo): psum.tile([P, hi - lo], F32, name="h_bank", tag=f"a{t}" if lo == 0 else "second_half")
+            for t, lo, hi in h_groups
+        }
 
-        def h_pass(u, t, m, words, scales):
+        def h_pass(t, lo, hi, m, words, scales):
             nc.tensor.matmul_mx(
-                out=h_bank[u][t][:],
+                out=h_bank[t, lo][:],
                 lhsT=dw[m][:, P * t : P * (t + 1)].bitcast(FP8X4),
-                lhsT_scale=ds_plane[4 * m : P, P * t : P * (t + 1)],
-                rhs=words.bitcast(FP8X4),
-                rhs_scale=scales,
+                lhsT_scale=ds_plane[PACK * m : P, P * t : P * (t + 1)],
+                rhs=words[:, lo:hi].bitcast(FP8X4),
+                rhs_scale=scales[:, lo:hi],
                 start=(m == 1),
                 stop=(m == 0),
             )
 
-        for u in range(2):
-            for t in range(PACK):
-                cols = slice(u * HALF, (u + 1) * HALF)
-                h_pass(u, t, 1, xt_w[:, cols], xt_s[:, cols])
+        for t, lo, hi in h_groups:
+            h_pass(t, lo, hi, 1, xt_w, xt_s)
 
         h_win = [keep.tile([P, 2 * S], F32, name=f"h_win{t}") for t in range(PACK)]
         dt_n3 = [h_win[t][:, S:] for t in range(PACK)]
-        larger = shared.tile([P, PACK * S], F32, name="larger", offset=0)
+        larger = shared.tile([P, PACK * S], F32, name="larger", offset=LARGER_AT)
         z = [keep.tile([P, HALF, PACK], BF16, name=f"z{u}", align_bytes=64) for u in range(2)]
 
         def scatter(t, side):
             nc.scalar.activation(dt[t][:].indirect((n1_t, n2_t)[side][:]), haar[t][:, side, :], ACT.Copy)
 
         def fetch_n3(t, lo, hi):
-            nc.scalar.activation(dt_n3[t][:, lo:hi], dt[t][:].indirect(n3_t[:, lo // 16 : hi // 16]), ACT.Copy)
+            nc.scalar.activation(dt_n3[t][:, lo:hi], dt[t][:].indirect(n3_t[:, lo // GROUP : hi // GROUP]), ACT.Copy)
 
         def take_larger(t, lo, hi):
             nc.vector.tensor_tensor(larger[:, t * S + lo : t * S + hi], dt[t][:, lo:hi], dt_n3[t][:, lo:hi], ALU.max)
 
         def weigh(t, u):
-            nc.vector.tensor_scalar(z[u][:, :, t], larger[:, t * S + u * HALF : t * S + (u + 1) * HALF], gs_t[:, t : t + 1], None, ALU.mult)
+            cols = slice(t * S + u * HALF, t * S + (u + 1) * HALF)
+            nc.vector.tensor_scalar(z[u][:, :, t], larger[:, cols], gs_t[:, t : t + 1], None, ALU.mult)
 
-        scatter(0, 0)
-        scatter(1, 0)
-        scatter(0, 1)
-        scatter(1, 1)
+        for side in range(2):
+            scatter(0, side)
+            scatter(1, side)
         scatter(2, 0)
         fetch_n3(0, 0, S)
         scatter(2, 1)
         fetch_n3(1, 0, S)
-        scatter(3, 0)
+        scatter(LAST, 0)
         fetch_n3(2, 0, S)
-        scatter(3, 1)
-        fetch_n3(3, 0, HALF)
-        fetch_n3(3, HALF, S)
-        for t in range(PACK - 1):
+        scatter(LAST, 1)
+        for u in range(2):
+            fetch_n3(LAST, u * HALF, (u + 1) * HALF)
+        for t in range(LAST):
             take_larger(t, 0, S)
             weigh(t, 0)
             weigh(t, 1)
-        take_larger(3, 0, HALF)
-        take_larger(3, HALF, S)
-        weigh(3, 0)
-        weigh(3, 1)
-
-        z_mx = []
         for u in range(2):
-            z_w = keep.tile([P, HALF], U32, name=f"z_w{u}", align_bytes=64)
-            z_s = keep.tile([P, HALF], U8, name=f"z_s{u}", align_bytes=64)
-            nc.vector.quantize_mx(out=z_w[:].bitcast(FP8X4), scales=z_s[:], in_=z[u][:].rearrange("p c t -> p (c t)"))
-            z_mx.append((z_w, z_s))
-        for t in range(PACK):
-            for u in range(2):
-                h_pass(u, t, 0, z_mx[u][0][:], z_mx[u][1][:])
-                cols = slice(u * HALF, (u + 1) * HALF)
-                if t == 0:
-                    nc.scalar.activation(h_win[t][:, cols], h_bank[u][t][:], ACT.Copy, scale=0.0625)
-                else:
-                    nc.vector.tensor_scalar(h_win[t][:, cols], h_bank[u][t][:], 0.0625, None, ALU.mult)
+            take_larger(LAST, u * HALF, (u + 1) * HALF)
+        for u in range(2):
+            weigh(LAST, u)
+
+        z_w = keep.tile([P, S], U32, name="z_w", align_bytes=64)
+        z_s = keep.tile([P, S], U8, name="z_s", align_bytes=64)
+        for u in range(2):
+            cols = slice(u * HALF, (u + 1) * HALF)
+            nc.vector.quantize_mx(
+                out=z_w[:, cols].bitcast(FP8X4), scales=z_s[:, cols], in_=z[u][:].rearrange("p c t -> p (c t)")
+            )
+        for t, lo, hi in h_groups:
+            h_pass(t, lo, hi, 0, z_w, z_s)
+            if t == 0:
+                nc.scalar.activation(h_win[t][:, lo:hi], h_bank[t, lo][:], ACT.Copy, scale=0.0625)
+            else:
+                nc.vector.tensor_scalar(h_win[t][:, lo:hi], h_bank[t, lo][:], 0.0625, None, ALU.mult)
 
         out_rows = out.rearrange("(p t) c -> p t c", t=PACK)
         st_win = [keep.tile([P, 2 * S], F32, name=f"st_win{t}") for t in range(PACK)]
@@ -237,7 +255,7 @@ def tile_picked_cmixhaarhehq_none_p_kernel(
         def finish(t, lo, hi):
             sg = keep.tile([P, hi - lo], F32, name=f"sg{t}_{lo}")
             nc.scalar.activation(
-                sg[:], st_win[t][:].indirect(n5_t[:, lo // 16 : hi // 16]), ACT.Sigmoid,
+                sg[:], st_win[t][:].indirect(n5_t[:, lo // GROUP : hi // GROUP]), ACT.Sigmoid,
                 bias=neg_bias[:, t : t + 1], scale=sl_t[:, t : t + 1],
             )
             res = keep.tile([P, hi - lo], F32, name=f"res{t}_{lo}")
@@ -245,8 +263,8 @@ def tile_picked_cmixhaarhehq_none_p_kernel(
             nc.sync.dma_start(out_rows[:, t, lo:hi], res[:])
 
         make_st(0)
-        for t in range(PACK - 1):
+        for t in range(LAST):
             make_st(t + 1)
             finish(t, 0, S)
-        finish(PACK - 1, 0, HALF)
-        finish(PACK - 1, HALF, S)
+        finish(LAST, 0, HALF)
+        finish(LAST, HALF, S)

from contextlib import ExitStack

import concourse.mybir as mybir

FLOPS = 402653184

F32 = mybir.dt.float32
BF16 = mybir.dt.bfloat16
I32 = mybir.dt.int32
U32 = mybir.dt.uint32
U16 = mybir.dt.uint16
U8 = mybir.dt.uint8
FP8X4 = mybir.dt.float8_e4m3fn_x4
FP4X4 = mybir.dt.float4_e2m1fn_x4
ALU = mybir.AluOpType
ACT = mybir.ActivationFunctionType

P = 128
PACK = 4
T, S, H, W, G = 1024, 256, 512, 128, 2048
HALF = S // 2
LAST = PACK - 1
QUADRANT = 32
GROUP = 16
LINE = 16
XS_ZEROED_BY_VECTOR = 384

DS_MOVED_AT = LARGER_AT = 0
DW_GOT_AT = (512, 2560)
DS_GOT_AT = (4608, 5632)
Y_AT = (8192, DS_GOT_AT[0], DS_GOT_AT[1], 2048)
W1S_RAW_AT = XT_S_AT = 6656
XT_W_AT = XT_S_AT + S


def tile_picked_cmixhaarhehq_none_p_kernel(
    tc, x_words, x_scales, w1_words, w1_scales, gs, d_words, d_scales, sl, th,
    offs, n1, n2, n3, k1, k2, two, n4, n5, out,
):
    nc = tc.nc
    with ExitStack() as ctx:
        lists = ctx.enter_context(tc.tile_pool(name="lists", bufs=1))
        keep = ctx.enter_context(tc.tile_pool(name="keep", bufs=1))
        shared = ctx.enter_context(tc.tile_pool(name="shared", bufs=1))
        psum = ctx.enter_context(tc.psum_pool(name="psum", bufs=1))

        def load_list(src, name):
            tile = lists.tile([P, src.shape[1]], U16, name=name)
            nc.sync.dma_start(tile[:], src)
            return tile

        def load_rows(src, name):
            tile = keep.tile([P, PACK], F32, name=name)
            nc.sync.dma_start(tile[:], src.rearrange("(p t) o -> p (t o)", t=PACK))
            return tile

        def load_scale_rows(queue, tile, scales, q):
            rows = tile[QUADRANT * q : QUADRANT * q + PACK, :]
            queue.dma_start(rows.bitcast(I32), scales[0, PACK * q : PACK * (q + 1), :].bitcast(I32))

        def deal(engine_copy, dst, src, run):
            engine_copy(
                dst.rearrange("p (t b i) -> p b t i", t=PACK, i=run),
                src.rearrange("p (b i t) -> p b t i", t=PACK, i=run),
            )

        xs_win = keep.tile([P, T], U8, name="xs_win")
        w1s_raw = shared.tile([P, H], U8, name="w1s_raw", offset=W1S_RAW_AT)
        ds_win = keep.tile([P, G], U8, name="ds_win")
        ds_moved = shared.tile([P, H], U8, name="ds_moved", offset=DS_MOVED_AT)
        nc.vector.memset(xs_win[:, :XS_ZEROED_BY_VECTOR].bitcast(I32), 0)
        nc.gpsimd.memset(xs_win[:, XS_ZEROED_BY_VECTOR:].bitcast(I32), 0)
        nc.vector.memset(w1s_raw[:].bitcast(I32), 0)

        offs_t = load_list(offs, "offs_t")
        two_t = load_list(two, "two_t")
        w1w_raw = keep.tile([P, 2 * H], U8, name="w1w_raw")
        nc.sync.dma_start(w1w_raw[:].bitcast(I32), w1_words[0].bitcast(I32))
        n1_t = load_list(n1, "n1_t")
        xw_win = keep.tile([P, T], U32, name="xw_win")
        nc.sync.dma_start(xw_win[:].bitcast(I32), x_words[0].rearrange("p n t -> p (n t)").bitcast(I32))
        for q in range(PACK):
            load_scale_rows(nc.sync if q == 0 else nc.scalar, xs_win, x_scales, q)
        for q in range(PACK):
            load_scale_rows(nc.sync, w1s_raw, w1_scales, q)
        n2_t = load_list(n2, "n2_t")
        nc.vector.memset(ds_win[:].bitcast(I32), 0)
        nc.vector.memset(ds_moved[:].bitcast(I32), 0)
        nc.sync.dma_start(ds_win[0:P:8, :].bitcast(I32), d_scales[0].bitcast(I32))
        k1_t = load_list(k1, "k1_t")
        k2_t = load_list(k2, "k2_t")
        n3_t = load_list(n3, "n3_t")
        gs_t = load_rows(gs, "gs_t")
        dw_win = keep.tile([P, G], U32, name="dw_win")
        nc.sync.dma_start(dw_win[:].bitcast(I32), d_words[0].rearrange("p n t -> p (n t)").bitcast(I32))
        n4_t = load_list(n4, "n4_t")
        n5_t = load_list(n5, "n5_t")
        sl_t = load_rows(sl, "sl_t")
        th_t = load_rows(th, "th_t")

        warm_in = keep.tile([P, 1], F32, name="warm_in")
        warm_out = keep.tile([P, 1], F32, name="warm_out")
        nc.gpsimd.memset(warm_in[:], 0.0)
        nc.scalar.activation(warm_out[:], warm_in[:], ACT.Sigmoid)

        w1w = keep.tile([P, 2 * H], U8, name="w1w", align_bytes=64)
        deal(nc.scalar.copy, w1w[:].bitcast(U16), w1w_raw[:].bitcast(U16), LINE // 2)
        w1s_first = keep.tile([P, P], U8, name="w1s_first", align_bytes=64)
        w1s_rest = keep.tile([P, H - P], U8, name="w1s_rest", align_bytes=64)
        xq_s = keep.tile([P, S], U8, name="xq_s", align_bytes=64)
        xq_w = keep.tile([P, S], U32, name="xq_w", align_bytes=64)
        nc.vector.tensor_copy(xq_s[:], xs_win[:].indirect(offs_t[:]))
        xt_s = shared.tile([P, S], U8, name="xt_s", align_bytes=64, offset=XT_S_AT)
        xt_w = shared.tile([P, S], U32, name="xt_w", align_bytes=64, offset=XT_W_AT)
        nc.vector.tensor_copy(xq_w[:], xw_win[:].indirect(offs_t[:]))
        w1s_by_t = w1s_raw[:].rearrange("p (m t) -> p t m", t=PACK)
        nc.vector.tensor_copy(w1s_first[:], w1s_by_t[:, 0, :])
        nc.vector.tensor_copy(
            w1s_rest[:].rearrange("p (t b i) -> p b t i", t=PACK - 1, i=LINE),
            w1s_by_t[:, 1:, :].rearrange("p t (b i) -> p b t i", i=LINE),
        )

        y = []
        for t in range(PACK):
            bank = psum.tile([P, S], F32, name="y_bank", tag=f"a{t}")
            nc.tensor.matmul_mx(
                out=bank[:],
                lhsT=w1w[:, 2 * P * t : 2 * P * (t + 1)].bitcast(FP4X4),
                lhsT_scale=w1s_first[:] if t == 0 else w1s_rest[:, P * (t - 1) : P * t],
                rhs=xq_w[:].bitcast(FP8X4),
                rhs_scale=xq_s[:],
                start=True,
                stop=True,
            )
            y_t = shared.tile([P, S], F32, name=f"y{t}", offset=Y_AT[t])
            if t == 0:
                nc.scalar.copy(y_t[:], bank[:])
            else:
                nc.vector.tensor_copy(y_t[:], bank[:])
            y.append(y_t)

        haar = []
        dt = [keep.tile([P, 2 * S], F32, name=f"dt{t}") for t in range(PACK)]
        for t in range(PACK):
            pa, pb = dt[t][:, S : S + W], dt[t][:, S + W :]
            nc.scalar.activation(pa, y[t][:].indirect(n1_t[:]), ACT.Copy)
            nc.scalar.activation(pb, y[t][:].indirect(n2_t[:]), ACT.Copy)
            haar_t = keep.tile([P, 2, W], F32, name=f"haar{t}")
            nc.vector.tensor_tensor(haar_t[:, 0, :], pa, pb, ALU.add)
            nc.vector.tensor_tensor(haar_t[:, 1, :], pa, pb, ALU.subtract)
            haar.append(haar_t)

        nc.vector.tensor_copy(xt_w[:], xw_win[:].indirect(two_t[:]))
        nc.vector.tensor_copy(xt_s[:], xs_win[:].indirect(two_t[:]))

        for m, k_t in enumerate((k1_t, k2_t)):
            ds_got = shared.tile([P, H], U8, name=f"ds_got{m}", offset=DS_GOT_AT[m])
            nc.vector.tensor_copy(ds_got[:], ds_win[:].indirect(k_t[:]))
            for r in range(PACK):
                nc.sync.dma_start(
                    ds_moved[PACK * m + r : P : QUADRANT, :].bitcast(I32), ds_got[8 * r : P : QUADRANT, :].bitcast(I32)
                )
        dw = []
        for m, k_t in enumerate((k1_t, k2_t)):
            got = shared.tile([P, H], U32, name=f"dw_got{m}", offset=DW_GOT_AT[m])
            nc.vector.tensor_copy(got[:], dw_win[:].indirect(k_t[:]))
            dealt = keep.tile([P, H], U32, name=f"dw_dealt{m}", align_bytes=64)
            deal(nc.vector.tensor_copy, dealt[:], got[:], LINE // 4)
            dw.append(dealt)
        ds_plane = keep.tile([P, H], U8, name="ds_plane", align_bytes=64)
        deal(nc.vector.tensor_copy, ds_plane[:], ds_moved[:], LINE)
        neg_bias = keep.tile([P, PACK], F32, name="neg_bias")
        nc.vector.scalar_tensor_tensor(neg_bias[:], sl_t[:], -1.0, th_t[:], ALU.mult, ALU.mult)

        h_groups = [(0, 0, HALF), (0, HALF, S)] + [(t, 0, S) for t in range(1, PACK)]
        h_bank = {
            (t, lo): psum.tile([P, hi - lo], F32, name="h_bank", tag=f"a{t}" if lo == 0 else "second_half")
            for t, lo, hi in h_groups
        }

        def h_pass(t, lo, hi, m, words, scales):
            nc.tensor.matmul_mx(
                out=h_bank[t, lo][:],
                lhsT=dw[m][:, P * t : P * (t + 1)].bitcast(FP8X4),
                lhsT_scale=ds_plane[PACK * m : P, P * t : P * (t + 1)],
                rhs=words[:, lo:hi].bitcast(FP8X4),
                rhs_scale=scales[:, lo:hi],
                start=(m == 1),
                stop=(m == 0),
            )

        for t, lo, hi in h_groups:
            h_pass(t, lo, hi, 1, xt_w, xt_s)

        h_win = [keep.tile([P, 2 * S], F32, name=f"h_win{t}") for t in range(PACK)]
        dt_n3 = [h_win[t][:, S:] for t in range(PACK)]
        larger = shared.tile([P, PACK * S], F32, name="larger", offset=LARGER_AT)
        z = [keep.tile([P, HALF, PACK], BF16, name=f"z{u}", align_bytes=64) for u in range(2)]

        def scatter(t, side):
            nc.scalar.activation(dt[t][:].indirect((n1_t, n2_t)[side][:]), haar[t][:, side, :], ACT.Copy)

        def fetch_n3(t, lo, hi):
            nc.scalar.activation(dt_n3[t][:, lo:hi], dt[t][:].indirect(n3_t[:, lo // GROUP : hi // GROUP]), ACT.Copy)

        def take_larger(t, lo, hi):
            nc.vector.tensor_tensor(larger[:, t * S + lo : t * S + hi], dt[t][:, lo:hi], dt_n3[t][:, lo:hi], ALU.max)

        def weigh(t, u):
            cols = slice(t * S + u * HALF, t * S + (u + 1) * HALF)
            nc.vector.tensor_scalar(z[u][:, :, t], larger[:, cols], gs_t[:, t : t + 1], None, ALU.mult)

        for side in range(2):
            scatter(0, side)
            scatter(1, side)
        scatter(2, 0)
        fetch_n3(0, 0, S)
        scatter(2, 1)
        fetch_n3(1, 0, S)
        scatter(LAST, 0)
        fetch_n3(2, 0, S)
        scatter(LAST, 1)
        for u in range(2):
            fetch_n3(LAST, u * HALF, (u + 1) * HALF)
        for t in range(LAST):
            take_larger(t, 0, S)
            weigh(t, 0)
            weigh(t, 1)
        for u in range(2):
            take_larger(LAST, u * HALF, (u + 1) * HALF)
        for u in range(2):
            weigh(LAST, u)

        z_w = keep.tile([P, S], U32, name="z_w", align_bytes=64)
        z_s = keep.tile([P, S], U8, name="z_s", align_bytes=64)
        for u in range(2):
            cols = slice(u * HALF, (u + 1) * HALF)
            nc.vector.quantize_mx(
                out=z_w[:, cols].bitcast(FP8X4), scales=z_s[:, cols], in_=z[u][:].rearrange("p c t -> p (c t)")
            )
        for t, lo, hi in h_groups:
            h_pass(t, lo, hi, 0, z_w, z_s)
            if t == 0:
                nc.scalar.activation(h_win[t][:, lo:hi], h_bank[t, lo][:], ACT.Copy, scale=0.0625)
            else:
                nc.vector.tensor_scalar(h_win[t][:, lo:hi], h_bank[t, lo][:], 0.0625, None, ALU.mult)

        out_rows = out.rearrange("(p t) c -> p t c", t=PACK)
        st_win = [keep.tile([P, 2 * S], F32, name=f"st_win{t}") for t in range(PACK)]

        def make_st(t):
            nc.scalar.activation(st_win[t][:, S:], h_win[t][:].indirect(n4_t[:]), ACT.Copy)
            nc.vector.tensor_tensor(st_win[t][:, :S], h_win[t][:, :S], st_win[t][:, S:], ALU.subtract)

        def finish(t, lo, hi):
            sg = keep.tile([P, hi - lo], F32, name=f"sg{t}_{lo}")
            nc.scalar.activation(
                sg[:], st_win[t][:].indirect(n5_t[:, lo // GROUP : hi // GROUP]), ACT.Sigmoid,
                bias=neg_bias[:, t : t + 1], scale=sl_t[:, t : t + 1],
            )
            res = keep.tile([P, hi - lo], F32, name=f"res{t}_{lo}")
            nc.vector.tensor_tensor(res[:], h_win[t][:, lo:hi], sg[:], ALU.mult)
            nc.sync.dma_start(out_rows[:, t, lo:hi], res[:])

        make_st(0)
        for t in range(LAST):
            make_st(t + 1)
            finish(t, 0, S)
        finish(LAST, 0, HALF)
        finish(LAST, HALF, S)
